import numpy as np
import ml_dtypes

BF16 = ml_dtypes.bfloat16


def bf(x):
    return np.asarray(x, np.float32).astype(BF16)


def f32(x):
    return np.asarray(x, np.float32)


def f64(x):
    return np.asarray(x).astype(np.float64)


def striped(idx):
    return np.tile(idx.reshape(-1, 16).T, (8, 1))


S, K, H, M, N, E, Q = 256, 256, 256, 128, 256, 2, 128


def sigmoid(v):
    return 1.0 / (1.0 + np.exp(-v))


def setup_inputs():
    return {"base": bf(np.random.standard_normal((M, S))), "x": bf(np.random.standard_normal((K, N))), "w": bf(np.random.standard_normal((E, K, H)) / np.sqrt(K)), "b": f32(0.5 * np.random.standard_normal((H, E))), "w2": bf(1.5 * np.random.standard_normal((E, H, M)) / np.sqrt(H)), "c": f32(0.2 + 0.8 * np.random.random_sample((1, N))), "offs": striped(np.random.permutation(S))}


def reference(base, x, w, b, w2, c, offs):
    idx = offs[:16].T.reshape(-1)
    z = f64(base).copy()
    for e in range(E):
        t = f64(w)[e].T @ f64(x)[:, e * Q : (e + 1) * Q] + f64(b)[:, e : e + 1]
        t = t * sigmoid(t) * f64(c)[:, e * Q : (e + 1) * Q]
        z[:, idx[e * Q : (e + 1) * Q]] += f64(w2)[e].T @ t
    return z

@@ -1,0 +1,73 @@
+import concourse.mybir as mybir
+from concourse.masks import make_identity
+
+FLOPS = 2 * 256 * 256 * 256 + 2 * 256 * 256 * 128
+
+BF16, F32, U16 = mybir.dt.bfloat16, mybir.dt.float32, mybir.dt.uint16
+MULT = mybir.AluOpType.mult
+SILU = mybir.ActivationFunctionType.Silu
+
+P = 128
+S, K, H, M, N = 256, 256, 256, 128, 256
+EXPERTS = 2
+PIECE = N // EXPERTS
+KB, HB = K // P, H // P
+
+
+def tile_rows_ffnback_silu_kernel(tc, base, x, w, b, w2, c, offs, out):
+    nc = tc.nc
+    with (
+        tc.tile_pool(name="held", bufs=1) as held,
+        tc.psum_pool(name="psum", bufs=1) as psum,
+    ):
+        x_sb = held.tile([P, KB, N], BF16)
+        w_sb = held.tile([P, EXPERTS, KB, H], BF16)
+        w2_sb = held.tile([P, EXPERTS, HB, M], BF16)
+        b_sb = held.tile([P, HB, EXPERTS], F32)
+        base_sb = held.tile([P, S], BF16)
+        c_row = held.tile([1, N], F32)
+        offsets = held.tile([P, N // 16], U16)
+
+        nc.scalar.dma_start(c_row[:], c)
+        nc.scalar.dma_start(b_sb[:], b.rearrange("(p hb) e -> p hb e", hb=HB))
+        nc.sync.dma_start(x_sb[:], x.rearrange("(p kb) n -> p kb n", kb=KB))
+        for e in range(EXPERTS):
+            nc.sync.dma_start(w_sb[:, e], w[e].rearrange("(p kb) h -> p kb h", kb=KB))
+        nc.sync.dma_start(base_sb[:], base)
+        nc.sync.dma_start(w2_sb[:], w2.rearrange("e (p hb) m -> p e hb m", hb=HB))
+        nc.sync.dma_start(offsets[:], offs)
+
+        ident = held.tile([P, P], BF16)
+        make_identity(nc, ident[:])
+        ones = held.tile([1, P], F32)
+        nc.vector.memset(ones[:], 1.0)
+
+        c_all = psum.tile([P, N], F32)
+        nc.tensor.matmul(c_all[:], ones[:], c_row[:], start=True, stop=True)
+
+        h = held.tile([P, EXPERTS, HB, PIECE], BF16)
+        for e in range(EXPERTS):
+            entries = slice(e * PIECE, (e + 1) * PIECE)
+            for hb in range(HB):
+                t = psum.tile([P, PIECE], F32, name=f"t_{e}_{hb}")
+                for kb in range(KB):
+                    nc.tensor.matmul(
+                        t[:], w_sb[:, e, kb, hb::HB], x_sb[:, kb, entries], start=kb == 0, stop=kb == KB - 1
+                    )
+                activated = held.tile([P, PIECE], F32, name=f"activated_{e}_{hb}")
+                nc.scalar.activation(activated[:], t[:], SILU, bias=b_sb[:, hb, e : e + 1])
+                nc.vector.tensor_tensor(h[:, e, hb], activated[:], c_all[:, entries], MULT)
+
+        window = psum.tile([P, S], F32)
+        nc.tensor.matmul(window[:], ident[:], base_sb[:], start=True, stop=False)
+
+        list_columns = PIECE // 16
+        for e in range(EXPERTS):
+            piece = offsets[:, e * list_columns : (e + 1) * list_columns]
+            for hb in range(HB):
+                last = e == EXPERTS - 1 and hb == HB - 1
+                nc.tensor.matmul(window[:].indirect(piece), w2_sb[:, e, hb], h[:, e, hb], start=False, stop=last)
+
+        out_sb = held.tile([P, S], F32)
+        nc.vector.tensor_copy(out_sb[:], window[:])
+        nc.sync.dma_start(out, out_sb[:])

@@ -37,6 +37,11 @@ def tile_rows_ffnback_silu_kernel(tc, base, x, w, b, w2, c, offs, out):
         nc.sync.dma_start(w2_sb[:], w2.rearrange("e (p hb) m -> p e hb m", hb=HB))
         nc.sync.dma_start(offsets[:], offs)
 
+        zeros = held.tile([P, 1], F32)
+        nc.vector.memset(zeros[:], 0.0)
+        table_loaded = held.tile([P, 1], F32)
+        nc.scalar.activation(table_loaded[:], zeros[:], SILU, bias=zeros[:])
+
         ident = held.tile([P, P], BF16)
         make_identity(nc, ident[:])
         ones = held.tile([1, P], F32)

@@ -12,6 +12,8 @@ S, K, H, M, N = 256, 256, 256, 128, 256
 EXPERTS = 2
 PIECE = N // EXPERTS
 KB, HB = K // P, H // P
+WARM_COLUMNS = 256
+WARM_MATMULS = 6
 
 
 def tile_rows_ffnback_silu_kernel(tc, base, x, w, b, w2, c, offs, out):
@@ -41,6 +43,12 @@ def tile_rows_ffnback_silu_kernel(tc, base, x, w, b, w2, c, offs, out):
         nc.vector.memset(zeros[:], 0.0)
         table_loaded = held.tile([P, 1], F32)
         nc.scalar.activation(table_loaded[:], zeros[:], SILU, bias=zeros[:])
+
+        idle_work = held.tile([P, WARM_COLUMNS], BF16)
+        nc.vector.memset(idle_work[:], 0.0)
+        unread = psum.tile([P, WARM_COLUMNS], F32)
+        for i in range(WARM_MATMULS):
+            nc.tensor.matmul(unread[:], idle_work[:, 0:P], idle_work[:], start=True, stop=True)
 
         ident = held.tile([P, P], BF16)
         make_identity(nc, ident[:])

@@ -13,7 +13,7 @@ EXPERTS = 2
 PIECE = N // EXPERTS
 KB, HB = K // P, H // P
 WARM_COLUMNS = 256
-WARM_MATMULS = 6
+WARM_MATMULS = 8
 
 
 def tile_rows_ffnback_silu_kernel(tc, base, x, w, b, w2, c, offs, out):
@@ -31,10 +31,10 @@ def tile_rows_ffnback_silu_kernel(tc, base, x, w, b, w2, c, offs, out):
         offsets = held.tile([P, N // 16], U16)
 
         nc.scalar.dma_start(c_row[:], c)
-        nc.scalar.dma_start(b_sb[:], b.rearrange("(p hb) e -> p hb e", hb=HB))
         nc.sync.dma_start(x_sb[:], x.rearrange("(p kb) n -> p kb n", kb=KB))
-        for e in range(EXPERTS):
-            nc.sync.dma_start(w_sb[:, e], w[e].rearrange("(p kb) h -> p kb h", kb=KB))
+        nc.sync.dma_start(w_sb[:, 0], w[0].rearrange("(p kb) h -> p kb h", kb=KB))
+        nc.sync.dma_start(b_sb[:], b.rearrange("(p hb) e -> p hb e", hb=HB))
+        nc.sync.dma_start(w_sb[:, 1], w[1].rearrange("(p kb) h -> p kb h", kb=KB))
         nc.sync.dma_start(base_sb[:], base)
         nc.sync.dma_start(w2_sb[:], w2.rearrange("e (p hb) m -> p e hb m", hb=HB))
         nc.sync.dma_start(offsets[:], offs)
@@ -45,7 +45,7 @@ def tile_rows_ffnback_silu_kernel(tc, base, x, w, b, w2, c, offs, out):
         nc.scalar.activation(table_loaded[:], zeros[:], SILU, bias=zeros[:])
 
         idle_work = held.tile([P, WARM_COLUMNS], BF16)
-        nc.vector.memset(idle_work[:], 0.0)
+        nc.gpsimd.memset(idle_work[:], 0.0)
         unread = psum.tile([P, WARM_COLUMNS], F32)
         for i in range(WARM_MATMULS):
             nc.tensor.matmul(unread[:], idle_work[:, 0:P], idle_work[:], start=True, stop=True)

import concourse.mybir as mybir
from concourse.masks import make_identity

FLOPS = 2 * 256 * 256 * 256 + 2 * 256 * 256 * 128

BF16, F32, U16 = mybir.dt.bfloat16, mybir.dt.float32, mybir.dt.uint16
MULT = mybir.AluOpType.mult
SILU = mybir.ActivationFunctionType.Silu

P = 128
S, K, H, M, N = 256, 256, 256, 128, 256
EXPERTS = 2
PIECE = N // EXPERTS
KB, HB = K // P, H // P
WARM_COLUMNS = 256
WARM_MATMULS = 8


def tile_rows_ffnback_silu_kernel(tc, base, x, w, b, w2, c, offs, out):
    nc = tc.nc
    with (
        tc.tile_pool(name="held", bufs=1) as held,
        tc.psum_pool(name="psum", bufs=1) as psum,
    ):
        x_sb = held.tile([P, KB, N], BF16)
        w_sb = held.tile([P, EXPERTS, KB, H], BF16)
        w2_sb = held.tile([P, EXPERTS, HB, M], BF16)
        b_sb = held.tile([P, HB, EXPERTS], F32)
        base_sb = held.tile([P, S], BF16)
        c_row = held.tile([1, N], F32)
        offsets = held.tile([P, N // 16], U16)

        nc.scalar.dma_start(c_row[:], c)
        nc.sync.dma_start(x_sb[:], x.rearrange("(p kb) n -> p kb n", kb=KB))
        nc.sync.dma_start(w_sb[:, 0], w[0].rearrange("(p kb) h -> p kb h", kb=KB))
        nc.sync.dma_start(b_sb[:], b.rearrange("(p hb) e -> p hb e", hb=HB))
        nc.sync.dma_start(w_sb[:, 1], w[1].rearrange("(p kb) h -> p kb h", kb=KB))
        nc.sync.dma_start(base_sb[:], base)
        nc.sync.dma_start(w2_sb[:], w2.rearrange("e (p hb) m -> p e hb m", hb=HB))
        nc.sync.dma_start(offsets[:], offs)

        zeros = held.tile([P, 1], F32)
        nc.vector.memset(zeros[:], 0.0)
        table_loaded = held.tile([P, 1], F32)
        nc.scalar.activation(table_loaded[:], zeros[:], SILU, bias=zeros[:])

        idle_work = held.tile([P, WARM_COLUMNS], BF16)
        nc.gpsimd.memset(idle_work[:], 0.0)
        unread = psum.tile([P, WARM_COLUMNS], F32)
        for i in range(WARM_MATMULS):
            nc.tensor.matmul(unread[:], idle_work[:, 0:P], idle_work[:], start=True, stop=True)

        ident = held.tile([P, P], BF16)
        make_identity(nc, ident[:])
        ones = held.tile([1, P], F32)
        nc.vector.memset(ones[:], 1.0)

        c_all = psum.tile([P, N], F32)
        nc.tensor.matmul(c_all[:], ones[:], c_row[:], start=True, stop=True)

        h = held.tile([P, EXPERTS, HB, PIECE], BF16)
        for e in range(EXPERTS):
            entries = slice(e * PIECE, (e + 1) * PIECE)
            for hb in range(HB):
                t = psum.tile([P, PIECE], F32, name=f"t_{e}_{hb}")
                for kb in range(KB):
                    nc.tensor.matmul(
                        t[:], w_sb[:, e, kb, hb::HB], x_sb[:, kb, entries], start=kb == 0, stop=kb == KB - 1
                    )
                activated = held.tile([P, PIECE], F32, name=f"activated_{e}_{hb}")
                nc.scalar.activation(activated[:], t[:], SILU, bias=b_sb[:, hb, e : e + 1])
                nc.vector.tensor_tensor(h[:, e, hb], activated[:], c_all[:, entries], MULT)

        window = psum.tile([P, S], F32)
        nc.tensor.matmul(window[:], ident[:], base_sb[:], start=True, stop=False)

        list_columns = PIECE // 16
        for e in range(EXPERTS):
            piece = offsets[:, e * list_columns : (e + 1) * list_columns]
            for hb in range(HB):
                last = e == EXPERTS - 1 and hb == HB - 1
                nc.tensor.matmul(window[:].indirect(piece), w2_sb[:, e, hb], h[:, e, hb], start=False, stop=last)

        out_sb = held.tile([P, S], F32)
        nc.vector.tensor_copy(out_sb[:], window[:])
        nc.sync.dma_start(out, out_sb[:])
